import numpy as np
import ml_dtypes


def mxq(x, axis, fmt="e4m3"):
    dtype, down = {"e4m3": (ml_dtypes.float8_e4m3fn, 7), "e5m2": (ml_dtypes.float8_e5m2, 14)}[fmt]
    v = np.moveaxis(np.asarray(x, np.float32).astype(ml_dtypes.bfloat16).astype(np.float64), axis, -1)
    blocks = v.reshape(v.shape[:-1] + (-1, 32))
    amax = np.abs(blocks).max(-1, keepdims=True)
    byte = np.maximum(np.where(amax > 0, np.frexp(amax)[1] - 1 + 127, 0) - down, 1)
    scale = np.exp2(byte - 127.0)
    codes = (blocks / scale).astype(np.float32).astype(dtype).astype(np.float64)
    return np.moveaxis((codes * scale).reshape(v.shape), -1, axis)


WIDE = False


def mx_kscale(k):
    if not WIDE:
        return np.ones(k)
    levels = np.array([10, -10, 5, -5, 0])
    if k % 512:
        return np.exp2(np.random.permutation(np.resize(levels, k // 32))).repeat(32)
    a = np.empty((k // 512, 16))
    for p in range(k // 512):
        a[p, :8] = np.random.permutation(np.resize(levels, 8))
        for g in range(8):
            far = levels[np.abs(levels - a[p, g]) >= 10]
            a[p, g + 8] = far[np.random.randint(len(far))]
    return np.exp2(a.ravel()).repeat(32)


BF16 = ml_dtypes.bfloat16


def bf(x):
    return np.asarray(x, np.float32).astype(BF16)


def f64(x):
    return np.asarray(x).astype(np.float64)


E2M1 = np.array([0.0, 0.5, 1.0, 1.5, 2.0, 3.0, 4.0, 6.0, -0.0, -0.5, -1.0, -1.5, -2.0, -3.0, -4.0, -6.0])


def pack_weight(w, fmt):
    k, n = w.shape
    w = f64(bf(w)).reshape(k // 32, 32, n)
    amax = np.abs(w).max(1)
    if fmt == "e4m3":
        byte = np.frexp(amax)[1] - 1 + 127 - 7
    else:
        mant, ex = np.frexp(amax / 6.0)
        byte = np.where(mant > 0.5, ex, ex - 1) + 127
    byte = np.clip(np.where(amax > 0, byte, 1), 1, 254)
    scaled = (w * np.exp2(127.0 - byte)[:, None, :]).reshape(k, n).astype(np.float32)
    by_word = np.ascontiguousarray(scaled.reshape(k // 512, 128, 4, n).transpose(0, 1, 3, 2))
    if fmt == "e4m3":
        words = by_word.astype(ml_dtypes.float8_e4m3fn).view(np.uint8)
    else:
        c = by_word.astype(ml_dtypes.float4_e2m1fn).view(np.uint8) & 0xF
        words = c[..., 0::2] | (c[..., 1::2] << 4)
    return np.ascontiguousarray(words), np.ascontiguousarray(byte.astype(np.uint8).reshape(k // 512, 16, n))


def unpack_weight(words, scales, fmt):
    g, p, n, _ = words.shape
    if fmt == "e4m3":
        vals = np.ascontiguousarray(words).view(ml_dtypes.float8_e4m3fn).astype(np.float64)
    else:
        nib = np.empty((g, p, n, 4), np.uint8)
        nib[..., 0::2] = words & 0xF
        nib[..., 1::2] = words >> 4
        vals = E2M1[nib]
    vals = vals * np.repeat(np.exp2(scales.astype(np.float64) - 127.0), 8, axis=1)[..., None]
    return vals.transpose(0, 1, 3, 2).reshape(g * 512, n)
def pack4(w):
    words, scales = pack_weight(w, "e2m1")
    return words.reshape(words.shape[0], 128, -1), scales


def unpack4(words, scales):
    return unpack_weight(words.reshape(words.shape[0], 128, -1, 2), scales, "e2m1")


def planes(Y):
    n, m = Y.shape
    b = f64(bf(Y)).reshape(n // 32, 32, m)
    amax = np.abs(b).max(1)
    byte = np.clip(np.where(amax > 0, np.frexp(amax)[1] - 1 + 127 - 7, 1), 1, 254)
    codes = (b * np.exp2(127.0 - byte)[:, None, :]).reshape(n, m).astype(np.float32).astype(ml_dtypes.float8_e4m3fn).view(np.uint8)
    words = codes.reshape(n // 512, 128, 4, m).transpose(0, 1, 3, 2)
    return np.ascontiguousarray(words), np.ascontiguousarray(byte.astype(np.uint8).reshape(n // 512, 16, m))


S, F, L, R = 768, 1024, 2048, 1536

def setup_inputs():
    s = mx_kscale(F)
    t = mx_kscale(L)
    delays = np.random.randn(F, S) * s[:, None]
    conn = np.random.randn(F, L) / np.sqrt(F) * t[None, :] / s[:, None]
    slack = (0.1 + 0.3 * np.abs(np.random.randn(L))) * t
    flows = 1.5 * np.random.randn(L, R) / np.sqrt(L) / t[:, None]
    rate = np.exp(0.8 * np.random.randn(R))
    liability = np.exp(0.3 * np.random.randn(S))
    delay_words, delay_scales = pack_weight(delays, "e4m3")
    conn_words, conn_scales = pack4(conn)
    return {"delay_words": delay_words, "delay_scales": delay_scales,
            "conn_words": conn_words, "conn_scales": conn_scales,
            "slack": bf(slack), "flows": bf(flows),
            "rate": bf(rate), "liability": bf(liability)}

def reference(delay_words, delay_scales, conn_words, conn_scales, slack, flows, rate, liability):
    D = unpack_weight(delay_words, delay_scales, "e4m3")
    C = unpack4(conn_words, conn_scales)
    late = D.T @ C
    H = np.maximum(late - f64(slack)[None, :], 0.0)
    exposure = mxq(H, 1, "e4m3") @ mxq(f64(flows), 0, "e4m3")
    y = exposure * f64(rate)[None, :] * f64(liability)[:, None]
    Y = y.T
    words, scales = planes(Y)
    return y, words, scales

@@ -1,0 +1,389 @@
+from contextlib import ExitStack
+
+import concourse.mybir as mybir
+from concourse.masks import make_identity
+
+S, F, L, R = 768, 1024, 2048, 1536
+FLOPS = 2 * S * F * L + 2 * S * L * R
+
+F32 = mybir.dt.float32
+BF16 = mybir.dt.bfloat16
+I32 = mybir.dt.int32
+U32 = mybir.dt.uint32
+U8 = mybir.dt.uint8
+FP8X4 = mybir.dt.float8_e4m3fn_x4
+FP4X4 = mybir.dt.float4_e2m1fn_x4
+ALU = mybir.AluOpType
+ACT = mybir.ActivationFunctionType
+
+P = 128
+KP = 512
+F_PASSES = F // KP
+L_PASSES = L // KP
+R_GROUPS = R // KP
+S_TILES = S // P
+S_WIDE = 512
+S_REST = S - S_WIDE
+PASS_ORDER = (0, 1, 3, 2)
+
+
+def tile_missed_connection_compensation_h2_kernel(
+    tc, delay_words, delay_scales, conn_words, conn_scales, slack, flows, rate, liability, out_0, out_1, out_2
+):
+    nc = tc.nc
+    with ExitStack() as ctx:
+        keep = ctx.enter_context(tc.tile_pool(name="keep", bufs=1))
+        work = ctx.enter_context(tc.tile_pool(name="work", bufs=1))
+        psum = ctx.enter_context(tc.psum_pool(name="psum", bufs=8))
+        ctx.enter_context(tc.manual_schedule())
+
+        def kept(name, shape, dtype):
+            return keep.tile(shape, dtype, name=name, align_bytes=64)
+
+        def rotating(tag, bufs, shape, dtype):
+            return work.tile(shape, dtype, name=tag, tag=tag, bufs=bufs, align_bytes=64)
+
+        def bank(shape, dtype):
+            return psum.tile(shape, dtype, name="bank", tag="bank")
+
+        d_scale = kept("d_scale", [P, F_PASSES * S], U8)
+        c_scale_first = kept("c_scale_first", [P, F_PASSES, P], I32)
+        c_scale_later = kept("c_scale_later", [P, F_PASSES, (L_PASSES - 1) * P], I32)
+        d_wide = kept("d_wide", [P, F_PASSES, S_WIDE], U32)
+        d_rest = kept("d_rest", [P, F_PASSES, S_REST], U32)
+        c_raw = [rotating("slab", 18, [P, F_PASSES, 256], I32) for g in range(L_PASSES)]
+        c_codes = [kept("c_codes%d" % g, [P, F_PASSES * 1024], U8) for g in range(L_PASSES)]
+        c_scale = [kept("c_scale%d" % g, [P, F_PASSES * 512], U8) for g in range(L_PASSES)]
+        f_first = [kept("f_first%d" % g, [P, 4, KP], BF16) for g in range(L_PASSES)]
+        f_later = [kept("f_later%d" % g, [P, 4, R - KP], BF16) for g in range(L_PASSES)]
+        slack_rows = kept("slack_rows", [L_PASSES, KP], BF16)
+        liab_rows = kept("liab_rows", [P, P], BF16)
+        rows = kept("rows", [P, 4, P], BF16)
+        neg_slack = kept("neg_slack", [P, 4, L_PASSES], F32)
+        liab = kept("liab", [P, S_TILES], F32)
+        rate_all = kept("rate_all", [P, R], BF16)
+        ident_f32 = kept("ident_f32", [P, P], F32)
+        ident_bf16 = kept("ident_bf16", [P, P], BF16)
+
+        nc.vector.memset(c_scale_first[:], 0)
+        nc.vector.memset(d_scale[:].bitcast(I32), 0)
+        nc.vector.memset(c_scale_later[:], 0)
+        nc.vector.memset(rows[:], 0.0)
+        nc.vector.memset(liab_rows[:], 0.0)
+        make_identity(nc, ident_f32[:])
+        nc.gpsimd.dma_start(out=slack_rows[:], in_=slack.rearrange("(g k) -> g k", k=KP))
+        nc.scalar.activation(out=ident_bf16[:], in_=ident_f32[:], func=ACT.Relu)
+
+        d_words = delay_words.rearrange("g p n t -> p g (n t)").bitcast(I32)
+        c_words = conn_words.rearrange("g p b -> p g b").bitcast(I32)
+        f_rows = flows.rearrange("(g j t e) r -> g e j t r", g=L_PASSES, t=4, e=4)
+
+        def load_c(g):
+            nc.sync.dma_start(out=c_raw[g][:], in_=c_words[:, :, 256 * g : 256 * (g + 1)])
+
+        def load_f(tile, g, cols):
+            for e in range(4):
+                nc.sync.dma_start(out=tile[e:P:4, :, :], in_=f_rows[g, e, :, :, cols])
+
+        c_sc = conn_scales.rearrange("g q b -> q g b").bitcast(I32)
+        d_sc = delay_scales.rearrange("g q b -> q g b").bitcast(I32)
+
+        def load_scales(queue, plane, rows_hbm, q):
+            queue.dma_start(out=plane[32 * q : 32 * q + 4, :, :], in_=rows_hbm[4 * q : 4 * q + 4, :, :])
+
+        d_plane = d_scale[:].bitcast(I32).rearrange("p (g w) -> p g w", g=F_PASSES)
+        load_c(0)
+        nc.sync.dma_start(out=d_wide[:].bitcast(I32), in_=d_words[:, :, 0:S_WIDE])
+        for q in range(4):
+            load_scales(nc.sync, c_scale_first, c_sc[:, :, 0:P], q)
+        for q in range(4):
+            load_scales(nc.sync if q % 2 == 0 else nc.gpsimd, d_plane, d_sc, q)
+        load_f(f_first[0], 0, slice(0, KP))
+        for q in range(4):
+            load_scales(nc.sync, c_scale_later, c_sc[:, :, P:], q)
+        for g in range(1, L_PASSES):
+            load_c(g)
+            load_f(f_first[g], g, slice(0, KP))
+        nc.sync.dma_start(out=d_rest[:].bitcast(I32), in_=d_words[:, :, S_WIDE:S])
+        nc.sync.dma_start(out=liab_rows[0:S_TILES, :], in_=liability.rearrange("(i p) -> i p", p=P))
+        for g in range(L_PASSES):
+            load_f(f_later[g], g, slice(KP, R))
+            if g == 1:
+                nc.sync.dma_start(out=rate_all[:], in_=rate.partition_broadcast(P))
+
+        def turn_slack():
+            nc.vector.tensor_scalar(
+                out=rows[0:L_PASSES, :, :].rearrange("g t (j e) -> g t j e", e=4),
+                in0=slack_rows[:].rearrange("g (j t e) -> g t j e", t=4, e=4),
+                scalar1=-1.0,
+                scalar2=None,
+                op0=ALU.mult,
+            )
+            turned = bank([P, 4, P], BF16)
+            for t in range(4):
+                nc.tensor.transpose(turned[:, t, :], rows[:, t, :], ident_bf16[:])
+            nc.scalar.copy(out=neg_slack[:], in_=turned[:, :, 0:L_PASSES])
+
+        def turn_liability():
+            turned = bank([P, P], BF16)
+            nc.tensor.transpose(turned[:], liab_rows[:], ident_bf16[:])
+            nc.scalar.copy(out=liab[:], in_=turned[:, 0:S_TILES])
+
+        def permute_c(g):
+            raw_scale = c_scale_first[:] if g == 0 else c_scale_later[:, :, P * (g - 1) : P * g]
+            nc.vector.tensor_copy(
+                out=c_codes[g][:].bitcast(I32).rearrange("p (f t j h) -> p f t j h", f=F_PASSES, t=4, h=2),
+                in_=c_raw[g][:].rearrange("p f (j t h) -> p f t j h", t=4, h=2),
+            )
+            nc.vector.tensor_copy(
+                out=c_scale[g][:].bitcast(I32).rearrange("p (f t j) -> p f t j", f=F_PASSES, t=4),
+                in_=raw_scale.rearrange("p f (j t) -> p f t j", t=4),
+            )
+
+        def late_passes(acc, g, t, d_tile, d_col, s0, width):
+            for f in range(F_PASSES):
+                nc.tensor.matmul_mx(
+                    out=acc,
+                    lhsT=c_codes[g][:, 1024 * f + 256 * t : 1024 * f + 256 * (t + 1)].bitcast(FP4X4),
+                    lhsT_scale=c_scale[g][:, 512 * f + P * t : 512 * f + P * (t + 1)],
+                    rhs=d_tile[:, f, d_col : d_col + width].bitcast(FP8X4),
+                    rhs_scale=d_scale[:, S * f + s0 : S * f + s0 + width],
+                    start=(f == 0),
+                    stop=(f == F_PASSES - 1),
+                )
+
+        h_rows = {}
+
+        def late_wide(g):
+            h_rows[g, 0] = rotating("h_wide", 3, [P, 4, S_WIDE], BF16)
+            for t in range(4):
+                acc = bank([P, S_WIDE], F32)
+                late_passes(acc[:], g, t, d_wide, 0, 0, S_WIDE)
+                nc.scalar.activation(out=h_rows[g, 0][:, t, :], in_=acc[:], func=ACT.Relu, bias=neg_slack[:, t, g : g + 1])
+
+        def late_rest(g):
+            h_rows[g, 1] = rotating("h_rest", 4, [P, 4, S_REST], BF16)
+            for t0 in (0, 2):
+                acc = bank([P, 2, S_REST], F32)
+                for t in (t0, t0 + 1):
+                    for c in range(0, S_REST, P):
+                        late_passes(acc[:, t - t0, c : c + P], g, t, d_rest, c, S_WIDE + c, P)
+                for t in (t0, t0 + 1):
+                    nc.scalar.activation(
+                        out=h_rows[g, 1][:, t, :], in_=acc[:, t - t0, :], func=ACT.Relu, bias=neg_slack[:, t, g : g + 1]
+                    )
+
+        grouped = {}
+        codes = {}
+        scales = {}
+
+        def interleave(key, src, copy, tag, bufs):
+            width = src.shape[2]
+            grouped[key] = rotating(tag, bufs, [P, width * 4], BF16)
+            copy(
+                out=grouped[key][:].rearrange("p (c i t) -> p c t i", i=4, t=4),
+                in_=src.rearrange("p t (c i) -> p c t i", i=4),
+            )
+
+        def quantize(key):
+            width = grouped[key].shape[1] // 4
+            codes[key] = kept("codes_%s%d%d" % key, [P, width], U32)
+            scales[key] = kept("scales_%s%d%d" % key, [P, width], U8)
+            nc.vector.quantize_mx(out=codes[key][:].bitcast(FP8X4), scales=scales[key][:], in_=grouped[key][:])
+
+        def group_h(g, part, copy):
+            interleave(("h", g, part), h_rows[g, part][:], copy, "grouped_h", 3)
+
+        def group_f(g, rg, copy):
+            src = f_first[g][:] if rg == 0 else f_later[g][:, :, KP * (rg - 1) : KP * rg]
+            interleave(("f", g, rg), src, copy, "grouped_f", 4)
+
+        y = {}
+        exposure = {}
+
+        def product(i, rg):
+            exposure[i, rg] = bank([P, KP], F32)
+            part, col = (0, P * i) if P * i < S_WIDE else (1, P * i - S_WIDE)
+            for n, g in enumerate(PASS_ORDER):
+                nc.tensor.matmul_mx(
+                    out=exposure[i, rg][:],
+                    lhsT=codes["h", g, part][:, col : col + P].bitcast(FP8X4),
+                    lhsT_scale=scales["h", g, part][:, col : col + P],
+                    rhs=codes["f", g, rg][:].bitcast(FP8X4),
+                    rhs_scale=scales["f", g, rg][:],
+                    start=(n == 0),
+                    stop=(n == L_PASSES - 1),
+                )
+
+        def finish(i, rg):
+            y[i, rg] = rotating("slab", 18, [P, KP], F32)
+            nc.vector.scalar_tensor_tensor(
+                out=y[i, rg][:],
+                in0=exposure[i, rg][:],
+                scalar=liab[:, i : i + 1],
+                in1=rate_all[:, KP * rg : KP * (rg + 1)],
+                op0=ALU.mult,
+                op1=ALU.mult,
+            )
+            nc.sync.dma_start(out=out_0[P * i : P * (i + 1), KP * rg : KP * (rg + 1)], in_=y[i, rg][:])
+
+        y_bf16 = {}
+
+        def round_y(i, rg, copy):
+            y_bf16[i, rg] = rotating("y_bf16", 6, [P, KP], BF16)
+            copy(
+                out=y_bf16[i, rg][:].rearrange("s (u p e) -> s u p e", u=2, e=2),
+                in_=y[i, rg][:].rearrange("s (p u e) -> s u p e", u=2, e=2),
+            )
+
+        turned_y = {}
+        y_words = {}
+        y_codes = [kept("y_codes%d" % rg, [P, S], U32) for rg in range(R_GROUPS)]
+        y_scales = [kept("y_scales%d" % rg, [P, S], U8) for rg in range(R_GROUPS)]
+
+        def turn(i0, count, rg):
+            turned_y[i0, rg] = bank([P, count, 2, P], F32)
+            for ii in range(count):
+                words = y_bf16[i0 + ii, rg][:].bitcast(F32)
+                for u in range(2):
+                    nc.tensor.transpose(turned_y[i0, rg][:, ii, u, :], words[:, P * u : P * (u + 1)], ident_f32[:])
+
+        def collect(i0, rg, copy):
+            count = turned_y[i0, rg].shape[1]
+            y_words[i0, rg] = rotating("y_words", 4, [P, KP * count], BF16)
+            copy(
+                out=y_words[i0, rg][:].bitcast(F32).rearrange("p (i s u) -> p i s u", i=count, u=2),
+                in_=turned_y[i0, rg][:].rearrange("p i u s -> p i s u"),
+            )
+
+        plane_words = out_1.rearrange("g p m t -> g p (m t)").bitcast(I32)
+        plane_scales = out_2.bitcast(I32)
+
+        def quantize_y(i0, rg):
+            end = P * i0 + y_words[i0, rg].shape[1] // 4
+            cols = slice(P * i0, end)
+            nc.vector.quantize_mx(out=y_codes[rg][:, cols].bitcast(FP8X4), scales=y_scales[rg][:, cols], in_=y_words[i0, rg][:])
+            if rg == R_GROUPS - 1:
+                nc.sync.dma_start(out=plane_words[rg, :, cols], in_=y_codes[rg][:, cols].bitcast(I32))
+            elif end == S:
+                nc.sync.dma_start(out=plane_words[rg, :, :], in_=y_codes[rg][:].bitcast(I32))
+            if end == S:
+                for q in range(4):
+                    nc.sync.dma_start(
+                        out=plane_scales[rg, 4 * q : 4 * q + 4, :], in_=y_scales[rg][32 * q : 32 * q + 4, :].bitcast(I32)
+                    )
+
+        vec, act = nc.vector.tensor_copy, nc.scalar.copy
+
+        turn_slack()
+        permute_c(0)
+        group_f(0, 0, vec)
+        permute_c(1)
+        for g in range(L_PASSES):
+            late_wide(g)
+            quantize(("f", g, 0))
+            if g + 2 == L_PASSES - 1:
+                permute_c(g + 2)
+            if g + 1 < L_PASSES:
+                group_f(g + 1, 0, vec)
+            if g == 0:
+                permute_c(g + 2)
+            if g > 0:
+                quantize(("h", g - 1, 0))
+            group_h(g, 0, vec)
+        late_rest(0)
+        group_h(0, 1, vec)
+        quantize(("h", L_PASSES - 1, 0))
+        for g in range(1, L_PASSES):
+            late_rest(g)
+            group_h(g, 1, vec)
+            quantize(("h", g - 1, 1))
+        turn_liability()
+
+        group_f(0, 1, act)
+        group_f(3, 1, vec)
+        quantize(("h", 3, 1))
+        group_f(1, 1, act)
+        group_f(2, 1, act)
+        for i in range(S_TILES):
+            product(i, 0)
+        quantize(("f", 0, 1))
+        quantize(("f", 3, 1))
+        quantize(("f", 1, 1))
+        finish(0, 0)
+        finish(1, 0)
+        quantize(("f", 2, 1))
+        group_f(0, 2, act)
+        group_f(1, 2, act)
+        for i in range(2):
+            product(i, 1)
+            finish(i + 2, 0)
+        group_f(3, 2, vec)
+        group_f(2, 2, act)
+        quantize(("f", 0, 2))
+        for i in range(2, 4):
+            product(i, 1)
+            finish(i + 2, 0)
+        quantize(("f", 3, 2))
+        product(4, 1)
+        product(5, 1)
+        finish(0, 1)
+        quantize(("f", 1, 2))
+        round_y(0, 0, vec)
+        round_y(1, 0, vec)
+        finish(1, 1)
+        quantize(("f", 2, 2))
+        for i in range(2, S_TILES):
+            round_y(i, 0, act)
+        product(0, 2)
+        finish(2, 1)
+        finish(3, 1)
+        product(1, 2)
+        finish(4, 1)
+        finish(5, 1)
+        for i0 in (0, 2, 4):
+            turn(i0, 2, 0)
+        for i0 in (0, 2, 4):
+            collect(i0, 0, act)
+        for i in range(3):
+            round_y(i, 1, vec)
+        for i in range(3, S_TILES):
+            round_y(i, 1, act)
+        product(2, 2)
+        product(3, 2)
+        quantize_y(0, 0)
+        finish(0, 2)
+        quantize_y(2, 0)
+        finish(1, 2)
+        quantize_y(4, 0)
+        for i0 in (0, 2, 4):
+            turn(i0, 2, 1)
+        finish(2, 2)
+        round_y(0, 2, vec)
+        round_y(1, 2, vec)
+        finish(3, 2)
+        for i0 in (0, 2, 4):
+            collect(i0, 1, act)
+        product(4, 2)
+        product(5, 2)
+        round_y(2, 2, vec)
+        quantize_y(0, 1)
+        round_y(3, 2, act)
+        finish(4, 2)
+        quantize_y(2, 1)
+        round_y(4, 2, act)
+        quantize_y(4, 1)
+        finish(5, 2)
+        turn(0, 2, 2)
+        turn(2, 2, 2)
+        turn(4, 1, 2)
+        round_y(5, 2, vec)
+        collect(0, 2, act)
+        turn(5, 1, 2)
+        collect(2, 2, act)
+        quantize_y(0, 2)
+        collect(5, 2, vec)
+        collect(4, 2, act)
+        quantize_y(2, 2)
+        quantize_y(4, 2)
+        quantize_y(5, 2)

@@ -25,6 +25,8 @@ S_TILES = S // P
 S_WIDE = 512
 S_REST = S - S_WIDE
 PASS_ORDER = (0, 1, 3, 2)
+WARM_PASSES = 20
+HALF = KP // 2
 
 
 def tile_missed_connection_compensation_h2_kernel(
@@ -47,43 +49,58 @@ def tile_missed_connection_compensation_h2_kernel(
             return psum.tile(shape, dtype, name="bank", tag="bank")
 
         d_scale = kept("d_scale", [P, F_PASSES * S], U8)
-        c_scale_first = kept("c_scale_first", [P, F_PASSES, P], I32)
-        c_scale_later = kept("c_scale_later", [P, F_PASSES, (L_PASSES - 1) * P], I32)
+        c_scale_first = kept("c_scale_first", [P, F_PASSES, 2 * P], I32)
+        c_scale_later = kept("c_scale_later", [P, F_PASSES, 2 * P], I32)
         d_wide = kept("d_wide", [P, F_PASSES, S_WIDE], U32)
         d_rest = kept("d_rest", [P, F_PASSES, S_REST], U32)
         c_raw = [rotating("slab", 18, [P, F_PASSES, 256], I32) for g in range(L_PASSES)]
         c_codes = [kept("c_codes%d" % g, [P, F_PASSES * 1024], U8) for g in range(L_PASSES)]
         c_scale = [kept("c_scale%d" % g, [P, F_PASSES * 512], U8) for g in range(L_PASSES)]
-        f_first = [kept("f_first%d" % g, [P, 4, KP], BF16) for g in range(L_PASSES)]
-        f_later = [kept("f_later%d" % g, [P, 4, R - KP], BF16) for g in range(L_PASSES)]
+        f_raw = {(g, rg): kept("f_raw%d%d" % (g, rg), [P, 4, KP], BF16) for g in range(L_PASSES) for rg in range(R_GROUPS)}
         slack_rows = kept("slack_rows", [L_PASSES, KP], BF16)
         liab_rows = kept("liab_rows", [P, P], BF16)
         rows = kept("rows", [P, 4, P], BF16)
         neg_slack = kept("neg_slack", [P, 4, L_PASSES], F32)
         liab = kept("liab", [P, S_TILES], F32)
-        rate_all = kept("rate_all", [P, R], BF16)
+        rate_first = kept("rate_first", [P, KP], BF16)
+        rate_later = kept("rate_later", [P, R - KP], BF16)
+        warm_codes = kept("warm_codes", [P, P], U32)
+        warm_scales = kept("warm_scales", [P, P], U8)
         ident_f32 = kept("ident_f32", [P, P], F32)
         ident_bf16 = kept("ident_bf16", [P, P], BF16)
 
-        nc.vector.memset(c_scale_first[:], 0)
         nc.vector.memset(d_scale[:].bitcast(I32), 0)
-        nc.vector.memset(c_scale_later[:], 0)
+        nc.vector.memset(c_scale_first[:], 0)
         nc.vector.memset(rows[:], 0.0)
+        nc.vector.memset(c_scale_later[:], 0)
+        nc.vector.quantize_mx(
+            out=warm_codes[:].bitcast(FP8X4), scales=warm_scales[:], in_=rows[:].rearrange("p t m -> p (t m)")
+        )
         nc.vector.memset(liab_rows[:], 0.0)
-        make_identity(nc, ident_f32[:])
         nc.gpsimd.dma_start(out=slack_rows[:], in_=slack.rearrange("(g k) -> g k", k=KP))
-        nc.scalar.activation(out=ident_bf16[:], in_=ident_f32[:], func=ACT.Relu)
+        for n in range(0, WARM_PASSES, 4):
+            warm = bank([P, 4, P], F32)
+            for j in range(4):
+                nc.tensor.matmul_mx(
+                    out=warm[:, j, :],
+                    lhsT=warm_codes[:].bitcast(FP8X4),
+                    lhsT_scale=warm_scales[:],
+                    rhs=warm_codes[:].bitcast(FP8X4),
+                    rhs_scale=warm_scales[:],
+                    start=True,
+                    stop=True,
+                )
 
         d_words = delay_words.rearrange("g p n t -> p g (n t)").bitcast(I32)
         c_words = conn_words.rearrange("g p b -> p g b").bitcast(I32)
         f_rows = flows.rearrange("(g j t e) r -> g e j t r", g=L_PASSES, t=4, e=4)
 
-        def load_c(g):
-            nc.sync.dma_start(out=c_raw[g][:], in_=c_words[:, :, 256 * g : 256 * (g + 1)])
+        def load_c(queue, g):
+            queue.dma_start(out=c_raw[g][:], in_=c_words[:, :, 256 * g : 256 * (g + 1)])
 
-        def load_f(tile, g, cols):
+        def load_f(g, rg):
             for e in range(4):
-                nc.sync.dma_start(out=tile[e:P:4, :, :], in_=f_rows[g, e, :, :, cols])
+                nc.sync.dma_start(out=f_raw[g, rg][e:P:4, :, :], in_=f_rows[g, e, :, :, KP * rg : KP * (rg + 1)])
 
         c_sc = conn_scales.rearrange("g q b -> q g b").bitcast(I32)
         d_sc = delay_scales.rearrange("g q b -> q g b").bitcast(I32)
@@ -92,24 +109,32 @@ def tile_missed_connection_compensation_h2_kernel(
             queue.dma_start(out=plane[32 * q : 32 * q + 4, :, :], in_=rows_hbm[4 * q : 4 * q + 4, :, :])
 
         d_plane = d_scale[:].bitcast(I32).rearrange("p (g w) -> p g w", g=F_PASSES)
-        load_c(0)
-        nc.sync.dma_start(out=d_wide[:].bitcast(I32), in_=d_words[:, :, 0:S_WIDE])
+        for q in range(2):
+            load_scales(nc.sync, d_plane, d_sc, q)
         for q in range(4):
-            load_scales(nc.sync, c_scale_first, c_sc[:, :, 0:P], q)
+            load_scales(nc.sync, c_scale_first, c_sc[:, :, 0 : 2 * P], q)
+        load_c(nc.scalar, 0)
+        nc.scalar.dma_start(out=d_wide[:].bitcast(I32), in_=d_words[:, :, 0:S_WIDE])
+        for q in range(2, 4):
+            load_scales(nc.gpsimd, d_plane, d_sc, q)
+        make_identity(nc, ident_f32[:])
         for q in range(4):
-            load_scales(nc.sync if q % 2 == 0 else nc.gpsimd, d_plane, d_sc, q)
-        load_f(f_first[0], 0, slice(0, KP))
-        for q in range(4):
-            load_scales(nc.sync, c_scale_later, c_sc[:, :, P:], q)
+            load_scales(nc.gpsimd, c_scale_later, c_sc[:, :, 2 * P :], q)
+        nc.scalar.activation(out=ident_bf16[:], in_=ident_f32[:], func=ACT.Relu)
+        load_c(nc.sync, 1)
+        load_f(0, 0)
+        load_c(nc.sync, 2)
+        load_c(nc.sync, 3)
         for g in range(1, L_PASSES):
-            load_c(g)
-            load_f(f_first[g], g, slice(0, KP))
+            load_f(g, 0)
         nc.sync.dma_start(out=d_rest[:].bitcast(I32), in_=d_words[:, :, S_WIDE:S])
         nc.sync.dma_start(out=liab_rows[0:S_TILES, :], in_=liability.rearrange("(i p) -> i p", p=P))
-        for g in range(L_PASSES):
-            load_f(f_later[g], g, slice(KP, R))
-            if g == 1:
-                nc.sync.dma_start(out=rate_all[:], in_=rate.partition_broadcast(P))
+        for g in PASS_ORDER:
+            load_f(g, 1)
+        nc.sync.dma_start(out=rate_first[:], in_=rate[0:KP].partition_broadcast(P))
+        for g in PASS_ORDER:
+            load_f(g, 2)
+        nc.sync.dma_start(out=rate_later[:], in_=rate[KP:R].partition_broadcast(P))
 
         def turn_slack():
             nc.vector.tensor_scalar(
@@ -130,7 +155,7 @@ def tile_missed_connection_compensation_h2_kernel(
             nc.scalar.copy(out=liab[:], in_=turned[:, 0:S_TILES])
 
         def permute_c(g):
-            raw_scale = c_scale_first[:] if g == 0 else c_scale_later[:, :, P * (g - 1) : P * g]
+            raw_scale = (c_scale_first if g < 2 else c_scale_later)[:, :, P * (g % 2) : P * (g % 2 + 1)]
             nc.vector.tensor_copy(
                 out=c_codes[g][:].bitcast(I32).rearrange("p (f t j h) -> p f t j h", f=F_PASSES, t=4, h=2),
                 in_=c_raw[g][:].rearrange("p f (j t h) -> p f t j h", t=4, h=2),
@@ -195,45 +220,48 @@ def tile_missed_connection_compensation_h2_kernel(
             interleave(("h", g, part), h_rows[g, part][:], copy, "grouped_h", 3)
 
         def group_f(g, rg, copy):
-            src = f_first[g][:] if rg == 0 else f_later[g][:, :, KP * (rg - 1) : KP * rg]
-            interleave(("f", g, rg), src, copy, "grouped_f", 4)
+            interleave(("f", g, rg), f_raw[g, rg][:], copy, "grouped_f", 4)
 
         y = {}
         exposure = {}
 
-        def product(i, rg):
-            exposure[i, rg] = bank([P, KP], F32)
+        def product(i, rg, c0=0, width=KP):
+            exposure[i, rg, c0] = bank([P, width], F32)
             part, col = (0, P * i) if P * i < S_WIDE else (1, P * i - S_WIDE)
             for n, g in enumerate(PASS_ORDER):
                 nc.tensor.matmul_mx(
-                    out=exposure[i, rg][:],
+                    out=exposure[i, rg, c0][:],
                     lhsT=codes["h", g, part][:, col : col + P].bitcast(FP8X4),
                     lhsT_scale=scales["h", g, part][:, col : col + P],
-                    rhs=codes["f", g, rg][:].bitcast(FP8X4),
-                    rhs_scale=scales["f", g, rg][:],
+                    rhs=codes["f", g, rg][:, c0 : c0 + width].bitcast(FP8X4),
+                    rhs_scale=scales["f", g, rg][:, c0 : c0 + width],
                     start=(n == 0),
                     stop=(n == L_PASSES - 1),
                 )
 
-        def finish(i, rg):
-            y[i, rg] = rotating("slab", 18, [P, KP], F32)
+        def finish(i, rg, c0=0, width=KP):
+            if c0 == 0:
+                y[i, rg] = rotating("slab", 18, [P, KP], F32)
+            rate_rg = rate_first[:] if rg == 0 else rate_later[:, KP * (rg - 1) : KP * rg]
             nc.vector.scalar_tensor_tensor(
-                out=y[i, rg][:],
-                in0=exposure[i, rg][:],
+                out=y[i, rg][:, c0 : c0 + width],
+                in0=exposure[i, rg, c0][:],
                 scalar=liab[:, i : i + 1],
-                in1=rate_all[:, KP * rg : KP * (rg + 1)],
+                in1=rate_rg[:, c0 : c0 + width],
                 op0=ALU.mult,
                 op1=ALU.mult,
             )
-            nc.sync.dma_start(out=out_0[P * i : P * (i + 1), KP * rg : KP * (rg + 1)], in_=y[i, rg][:])
+            if c0 + width == KP:
+                nc.sync.dma_start(out=out_0[P * i : P * (i + 1), KP * rg : KP * (rg + 1)], in_=y[i, rg][:])
 
         y_bf16 = {}
 
-        def round_y(i, rg, copy):
-            y_bf16[i, rg] = rotating("y_bf16", 6, [P, KP], BF16)
+        def round_y(i, rg, copy, c0=0, width=KP):
+            if c0 == 0:
+                y_bf16[i, rg] = rotating("y_bf16", 8, [P, 2, P, 2], BF16)
             copy(
-                out=y_bf16[i, rg][:].rearrange("s (u p e) -> s u p e", u=2, e=2),
-                in_=y[i, rg][:].rearrange("s (p u e) -> s u p e", u=2, e=2),
+                out=y_bf16[i, rg][:, :, c0 // 4 : (c0 + width) // 4, :],
+                in_=y[i, rg][:, c0 : c0 + width].rearrange("s (p u e) -> s u p e", u=2, e=2),
             )
 
         turned_y = {}
@@ -244,15 +272,17 @@ def tile_missed_connection_compensation_h2_kernel(
         def turn(i0, count, rg):
             turned_y[i0, rg] = bank([P, count, 2, P], F32)
             for ii in range(count):
-                words = y_bf16[i0 + ii, rg][:].bitcast(F32)
+                words = y_bf16[i0 + ii, rg][:].rearrange("s u p e -> s (u p e)").bitcast(F32)
                 for u in range(2):
                     nc.tensor.transpose(turned_y[i0, rg][:, ii, u, :], words[:, P * u : P * (u + 1)], ident_f32[:])
 
         def collect(i0, rg, copy):
             count = turned_y[i0, rg].shape[1]
-            y_words[i0, rg] = rotating("y_words", 4, [P, KP * count], BF16)
+            if i0 % 2 == 0:
+                y_words[i0 // 2, rg] = rotating("y_words", 4, [P, 2 * KP], BF16)
+            c0 = KP * (i0 % 2)
             copy(
-                out=y_words[i0, rg][:].bitcast(F32).rearrange("p (i s u) -> p i s u", i=count, u=2),
+                out=y_words[i0 // 2, rg][:, c0 : c0 + KP * count].bitcast(F32).rearrange("p (i s u) -> p i s u", i=count, u=2),
                 in_=turned_y[i0, rg][:].rearrange("p i u s -> p i s u"),
             )
 
@@ -260,77 +290,78 @@ def tile_missed_connection_compensation_h2_kernel(
         plane_scales = out_2.bitcast(I32)
 
         def quantize_y(i0, rg):
-            end = P * i0 + y_words[i0, rg].shape[1] // 4
-            cols = slice(P * i0, end)
-            nc.vector.quantize_mx(out=y_codes[rg][:, cols].bitcast(FP8X4), scales=y_scales[rg][:, cols], in_=y_words[i0, rg][:])
-            if rg == R_GROUPS - 1:
-                nc.sync.dma_start(out=plane_words[rg, :, cols], in_=y_codes[rg][:, cols].bitcast(I32))
-            elif end == S:
-                nc.sync.dma_start(out=plane_words[rg, :, :], in_=y_codes[rg][:].bitcast(I32))
-            if end == S:
-                for q in range(4):
-                    nc.sync.dma_start(
-                        out=plane_scales[rg, 4 * q : 4 * q + 4, :], in_=y_scales[rg][32 * q : 32 * q + 4, :].bitcast(I32)
-                    )
+            cols = slice(P * i0, P * (i0 + 2))
+            nc.vector.quantize_mx(
+                out=y_codes[rg][:, cols].bitcast(FP8X4), scales=y_scales[rg][:, cols], in_=y_words[i0 // 2, rg][:]
+            )
+
+        def store_words(rg, i0, i1):
+            cols = slice(P * i0, P * i1)
+            nc.sync.dma_start(out=plane_words[rg, :, cols], in_=y_codes[rg][:, cols].bitcast(I32))
+
+        def store_scales(rg, queues):
+            for q in range(4):
+                queues[q % len(queues)].dma_start(
+                    out=plane_scales[rg, 4 * q : 4 * q + 4, :], in_=y_scales[rg][32 * q : 32 * q + 4, :].bitcast(I32)
+                )
 
         vec, act = nc.vector.tensor_copy, nc.scalar.copy
 
         turn_slack()
         permute_c(0)
-        group_f(0, 0, vec)
         permute_c(1)
-        for g in range(L_PASSES):
-            late_wide(g)
-            quantize(("f", g, 0))
-            if g + 2 == L_PASSES - 1:
-                permute_c(g + 2)
-            if g + 1 < L_PASSES:
-                group_f(g + 1, 0, vec)
-            if g == 0:
-                permute_c(g + 2)
-            if g > 0:
-                quantize(("h", g - 1, 0))
-            group_h(g, 0, vec)
-        late_rest(0)
-        group_h(0, 1, vec)
-        quantize(("h", L_PASSES - 1, 0))
+        group_f(0, 0, vec)
+        permute_c(2)
+        late_wide(0)
+        quantize(("f", 0, 0))
+        permute_c(3)
+        group_h(0, 0, vec)
         for g in range(1, L_PASSES):
+            late_wide(g)
+            if g < L_PASSES - 1:
+                group_f(g, 0, vec)
+            quantize(("h", g - 1, 0))
+            group_h(g, 0, vec)
+            if g < L_PASSES - 1:
+                quantize(("f", g, 0))
+        group_f(3, 0, act)
+        for g in range(L_PASSES):
             late_rest(g)
+        turn_liability()
+        quantize(("f", 3, 0))
+        quantize(("h", L_PASSES - 1, 0))
+        group_h(0, 1, vec)
+        group_f(0, 1, vec)
+        quantize(("h", 0, 1))
+        group_h(1, 1, vec)
+        quantize(("f", 0, 1))
+        for g in range(2, L_PASSES):
             group_h(g, 1, vec)
             quantize(("h", g - 1, 1))
-        turn_liability()
-
-        group_f(0, 1, act)
-        group_f(3, 1, vec)
+        group_f(3, 1, act)
         quantize(("h", 3, 1))
-        group_f(1, 1, act)
+        group_f(1, 1, vec)
         group_f(2, 1, act)
         for i in range(S_TILES):
             product(i, 0)
-        quantize(("f", 0, 1))
         quantize(("f", 3, 1))
         quantize(("f", 1, 1))
         finish(0, 0)
-        finish(1, 0)
         quantize(("f", 2, 1))
-        group_f(0, 2, act)
-        group_f(1, 2, act)
-        for i in range(2):
+        finish(1, 0)
+        for g in PASS_ORDER:
+            group_f(g, 2, act)
+        for i in range(4):
             product(i, 1)
             finish(i + 2, 0)
-        group_f(3, 2, vec)
-        group_f(2, 2, act)
-        quantize(("f", 0, 2))
-        for i in range(2, 4):
-            product(i, 1)
-            finish(i + 2, 0)
-        quantize(("f", 3, 2))
-        product(4, 1)
-        product(5, 1)
-        finish(0, 1)
-        quantize(("f", 1, 2))
+            if i % 2 == 1:
+                quantize(("f", PASS_ORDER[i // 2], 2))
         round_y(0, 0, vec)
         round_y(1, 0, vec)
+        product(4, 1)
+        product(5, 1)
+        quantize(("f", 3, 2))
+        finish(0, 1)
         finish(1, 1)
         quantize(("f", 2, 2))
         for i in range(2, S_TILES):
@@ -338,52 +369,61 @@ def tile_missed_connection_compensation_h2_kernel(
         product(0, 2)
         finish(2, 1)
         finish(3, 1)
-        product(1, 2)
         finish(4, 1)
-        finish(5, 1)
         for i0 in (0, 2, 4):
             turn(i0, 2, 0)
         for i0 in (0, 2, 4):
             collect(i0, 0, act)
-        for i in range(3):
-            round_y(i, 1, vec)
-        for i in range(3, S_TILES):
-            round_y(i, 1, act)
+        finish(5, 1)
+        round_y(0, 1, vec)
+        round_y(1, 1, vec)
+        product(1, 2)
         product(2, 2)
-        product(3, 2)
-        quantize_y(0, 0)
+        for i in range(2, S_TILES):
+            round_y(i, 1, act)
         finish(0, 2)
+        quantize_y(0, 0)
         quantize_y(2, 0)
         finish(1, 2)
         quantize_y(4, 0)
-        for i0 in (0, 2, 4):
-            turn(i0, 2, 1)
-        finish(2, 2)
+        store_words(0, 0, S_TILES)
+        store_scales(0, [nc.sync])
         round_y(0, 2, vec)
         round_y(1, 2, vec)
-        finish(3, 2)
+        product(3, 2)
+        for i0 in (0, 2, 4):
+            turn(i0, 2, 1)
+        turn(0, 2, 2)
+        finish(2, 2)
         for i0 in (0, 2, 4):
             collect(i0, 1, act)
+        collect(0, 2, act)
+        finish(3, 2)
         product(4, 2)
-        product(5, 2)
+        product(5, 2, 0, HALF)
+        product(5, 2, HALF, HALF)
         round_y(2, 2, vec)
+        round_y(3, 2, vec)
         quantize_y(0, 1)
-        round_y(3, 2, act)
-        finish(4, 2)
         quantize_y(2, 1)
-        round_y(4, 2, act)
         quantize_y(4, 1)
-        finish(5, 2)
-        turn(0, 2, 2)
+        store_words(1, 0, S_TILES)
+        store_scales(1, [nc.sync])
+        finish(4, 2)
+        round_y(4, 2, act)
+        finish(5, 2, 0, HALF)
+        finish(5, 2, HALF, HALF)
         turn(2, 2, 2)
         turn(4, 1, 2)
-        round_y(5, 2, vec)
-        collect(0, 2, act)
-        turn(5, 1, 2)
-        collect(2, 2, act)
+        round_y(5, 2, vec, 0, HALF)
+        round_y(5, 2, vec, HALF, HALF)
         quantize_y(0, 2)
-        collect(5, 2, vec)
-        collect(4, 2, act)
+        collect(2, 2, act)
+        turn(5, 1, 2)
+        collect(4, 2, vec)
+        collect(5, 2, act)
         quantize_y(2, 2)
+        store_words(2, 0, 4)
         quantize_y(4, 2)
-        quantize_y(5, 2)
+        store_words(2, 4, S_TILES)
+        store_scales(2, [nc.scalar, nc.sync])

@@ -25,7 +25,7 @@ S_TILES = S // P
 S_WIDE = 512
 S_REST = S - S_WIDE
 PASS_ORDER = (0, 1, 3, 2)
-WARM_PASSES = 20
+WARM_PASSES = 16
 HALF = KP // 2
 
 
@@ -69,13 +69,13 @@ def tile_missed_connection_compensation_h2_kernel(
         ident_f32 = kept("ident_f32", [P, P], F32)
         ident_bf16 = kept("ident_bf16", [P, P], BF16)
 
-        nc.vector.memset(d_scale[:].bitcast(I32), 0)
-        nc.vector.memset(c_scale_first[:], 0)
         nc.vector.memset(rows[:], 0.0)
-        nc.vector.memset(c_scale_later[:], 0)
+        nc.vector.memset(d_scale[:].bitcast(I32), 0)
         nc.vector.quantize_mx(
             out=warm_codes[:].bitcast(FP8X4), scales=warm_scales[:], in_=rows[:].rearrange("p t m -> p (t m)")
         )
+        nc.vector.memset(c_scale_first[:], 0)
+        nc.vector.memset(c_scale_later[:], 0)
         nc.vector.memset(liab_rows[:], 0.0)
         nc.gpsimd.dma_start(out=slack_rows[:], in_=slack.rearrange("(g k) -> g k", k=KP))
         for n in range(0, WARM_PASSES, 4):
@@ -105,24 +105,24 @@ def tile_missed_connection_compensation_h2_kernel(
         c_sc = conn_scales.rearrange("g q b -> q g b").bitcast(I32)
         d_sc = delay_scales.rearrange("g q b -> q g b").bitcast(I32)
 
-        def load_scales(queue, plane, rows_hbm, q):
-            queue.dma_start(out=plane[32 * q : 32 * q + 4, :, :], in_=rows_hbm[4 * q : 4 * q + 4, :, :])
+        def load_scales(plane, rows_hbm, r):
+            nc.sync.dma_start(out=plane[r:P:32, :, :], in_=rows_hbm[r:16:4, :, :])
 
         d_plane = d_scale[:].bitcast(I32).rearrange("p (g w) -> p g w", g=F_PASSES)
-        for q in range(2):
-            load_scales(nc.sync, d_plane, d_sc, q)
-        for q in range(4):
-            load_scales(nc.sync, c_scale_first, c_sc[:, :, 0 : 2 * P], q)
-        load_c(nc.scalar, 0)
-        nc.scalar.dma_start(out=d_wide[:].bitcast(I32), in_=d_words[:, :, 0:S_WIDE])
-        for q in range(2, 4):
-            load_scales(nc.gpsimd, d_plane, d_sc, q)
+        load_c(nc.sync, 0)
+        load_scales(d_plane, d_sc, 0)
+        nc.sync.dma_start(out=d_wide[:].bitcast(I32), in_=d_words[:, :, 0:S_WIDE])
+        load_scales(d_plane, d_sc, 1)
+        for r in range(4):
+            load_scales(c_scale_first, c_sc[:, :, 0 : 2 * P], r)
+        for r in range(2, 4):
+            load_scales(d_plane, d_sc, r)
         make_identity(nc, ident_f32[:])
-        for q in range(4):
-            load_scales(nc.gpsimd, c_scale_later, c_sc[:, :, 2 * P :], q)
         nc.scalar.activation(out=ident_bf16[:], in_=ident_f32[:], func=ACT.Relu)
         load_c(nc.sync, 1)
         load_f(0, 0)
+        for r in range(4):
+            load_scales(c_scale_later, c_sc[:, :, 2 * P :], r)
         load_c(nc.sync, 2)
         load_c(nc.sync, 3)
         for g in range(1, L_PASSES):
@@ -302,7 +302,7 @@ def tile_missed_connection_compensation_h2_kernel(
         def store_scales(rg, queues):
             for q in range(4):
                 queues[q % len(queues)].dma_start(
-                    out=plane_scales[rg, 4 * q : 4 * q + 4, :], in_=y_scales[rg][32 * q : 32 * q + 4, :].bitcast(I32)
+                    out=plane_scales[rg, q:16:4, :], in_=y_scales[rg][q:P:32, :].bitcast(I32)
                 )
 
         vec, act = nc.vector.tensor_copy, nc.scalar.copy
@@ -418,12 +418,13 @@ def tile_missed_connection_compensation_h2_kernel(
         round_y(5, 2, vec, 0, HALF)
         round_y(5, 2, vec, HALF, HALF)
         quantize_y(0, 2)
+        store_words(2, 0, 2)
         collect(2, 2, act)
         turn(5, 1, 2)
         collect(4, 2, vec)
         collect(5, 2, act)
         quantize_y(2, 2)
-        store_words(2, 0, 4)
+        store_words(2, 2, 4)
         quantize_y(4, 2)
         store_words(2, 4, S_TILES)
-        store_scales(2, [nc.scalar, nc.sync])
+        store_scales(2, [nc.sync])

@@ -24,8 +24,8 @@ R_GROUPS = R // KP
 S_TILES = S // P
 S_WIDE = 512
 S_REST = S - S_WIDE
-PASS_ORDER = (0, 1, 3, 2)
-WARM_PASSES = 16
+PASS_ORDER = (0, 1, 2, 3)
+WARM_PASSES = 12
 HALF = KP // 2
 
 
@@ -77,19 +77,22 @@ def tile_missed_connection_compensation_h2_kernel(
         nc.vector.memset(c_scale_first[:], 0)
         nc.vector.memset(c_scale_later[:], 0)
         nc.vector.memset(liab_rows[:], 0.0)
-        nc.gpsimd.dma_start(out=slack_rows[:], in_=slack.rearrange("(g k) -> g k", k=KP))
-        for n in range(0, WARM_PASSES, 4):
-            warm = bank([P, 4, P], F32)
-            for j in range(4):
-                nc.tensor.matmul_mx(
-                    out=warm[:, j, :],
-                    lhsT=warm_codes[:].bitcast(FP8X4),
-                    lhsT_scale=warm_scales[:],
-                    rhs=warm_codes[:].bitcast(FP8X4),
-                    rhs_scale=warm_scales[:],
-                    start=True,
-                    stop=True,
-                )
+        make_identity(nc, ident_f32[:])
+        nc.scalar.activation(out=ident_bf16[:], in_=ident_f32[:], func=ACT.Relu)
+
+        def warm_up():
+            for n in range(0, WARM_PASSES, 4):
+                warm = bank([P, 4, P], F32)
+                for j in range(4):
+                    nc.tensor.matmul_mx(
+                        out=warm[:, j, :],
+                        lhsT=warm_codes[:].bitcast(FP8X4),
+                        lhsT_scale=warm_scales[:],
+                        rhs=warm_codes[:].bitcast(FP8X4),
+                        rhs_scale=warm_scales[:],
+                        start=True,
+                        stop=True,
+                    )
 
         d_words = delay_words.rearrange("g p n t -> p g (n t)").bitcast(I32)
         c_words = conn_words.rearrange("g p b -> p g b").bitcast(I32)
@@ -109,6 +112,7 @@ def tile_missed_connection_compensation_h2_kernel(
             nc.sync.dma_start(out=plane[r:P:32, :, :], in_=rows_hbm[r:16:4, :, :])
 
         d_plane = d_scale[:].bitcast(I32).rearrange("p (g w) -> p g w", g=F_PASSES)
+        nc.sync.dma_start(out=slack_rows[:], in_=slack.rearrange("(g k) -> g k", k=KP))
         load_c(nc.sync, 0)
         load_scales(d_plane, d_sc, 0)
         nc.sync.dma_start(out=d_wide[:].bitcast(I32), in_=d_words[:, :, 0:S_WIDE])
@@ -117,17 +121,16 @@ def tile_missed_connection_compensation_h2_kernel(
             load_scales(c_scale_first, c_sc[:, :, 0 : 2 * P], r)
         for r in range(2, 4):
             load_scales(d_plane, d_sc, r)
-        make_identity(nc, ident_f32[:])
-        nc.scalar.activation(out=ident_bf16[:], in_=ident_f32[:], func=ACT.Relu)
         load_c(nc.sync, 1)
         load_f(0, 0)
         for r in range(4):
             load_scales(c_scale_later, c_sc[:, :, 2 * P :], r)
         load_c(nc.sync, 2)
         load_c(nc.sync, 3)
-        for g in range(1, L_PASSES):
-            load_f(g, 0)
+        load_f(1, 0)
         nc.sync.dma_start(out=d_rest[:].bitcast(I32), in_=d_words[:, :, S_WIDE:S])
+        load_f(2, 0)
+        load_f(3, 0)
         nc.sync.dma_start(out=liab_rows[0:S_TILES, :], in_=liability.rearrange("(i p) -> i p", p=P))
         for g in PASS_ORDER:
             load_f(g, 1)
@@ -154,16 +157,22 @@ def tile_missed_connection_compensation_h2_kernel(
             nc.tensor.transpose(turned[:], liab_rows[:], ident_bf16[:])
             nc.scalar.copy(out=liab[:], in_=turned[:, 0:S_TILES])
 
-        def permute_c(g):
+        def permute_scales(g):
             raw_scale = (c_scale_first if g < 2 else c_scale_later)[:, :, P * (g % 2) : P * (g % 2 + 1)]
-            nc.vector.tensor_copy(
-                out=c_codes[g][:].bitcast(I32).rearrange("p (f t j h) -> p f t j h", f=F_PASSES, t=4, h=2),
-                in_=c_raw[g][:].rearrange("p f (j t h) -> p f t j h", t=4, h=2),
-            )
             nc.vector.tensor_copy(
                 out=c_scale[g][:].bitcast(I32).rearrange("p (f t j) -> p f t j", f=F_PASSES, t=4),
                 in_=raw_scale.rearrange("p f (j t) -> p f t j", t=4),
             )
+
+        def permute_codes(g):
+            nc.vector.tensor_copy(
+                out=c_codes[g][:].bitcast(I32).rearrange("p (f t j h) -> p f t j h", f=F_PASSES, t=4, h=2),
+                in_=c_raw[g][:].rearrange("p f (j t h) -> p f t j h", t=4, h=2),
+            )
+
+        def permute_c(g):
+            permute_codes(g)
+            permute_scales(g)
 
         def late_passes(acc, g, t, d_tile, d_col, s0, width):
             for f in range(F_PASSES):
@@ -202,13 +211,14 @@ def tile_missed_connection_compensation_h2_kernel(
         codes = {}
         scales = {}
 
-        def interleave(key, src, copy, tag, bufs):
-            width = src.shape[2]
-            grouped[key] = rotating(tag, bufs, [P, width * 4], BF16)
-            copy(
-                out=grouped[key][:].rearrange("p (c i t) -> p c t i", i=4, t=4),
-                in_=src.rearrange("p t (c i) -> p c t i", i=4),
-            )
+        def interleave(key, src, copies, tag, bufs):
+            grouped[key] = rotating(tag, bufs, [P, src.shape[2] * 4], BF16)
+            width = src.shape[2] // len(copies)
+            for n, copy in enumerate(copies):
+                copy(
+                    out=grouped[key][:, 4 * width * n : 4 * width * (n + 1)].rearrange("p (c i t) -> p c t i", i=4, t=4),
+                    in_=src[:, :, width * n : width * (n + 1)].rearrange("p t (c i) -> p c t i", i=4),
+                )
 
         def quantize(key):
             width = grouped[key].shape[1] // 4
@@ -216,11 +226,11 @@ def tile_missed_connection_compensation_h2_kernel(
             scales[key] = kept("scales_%s%d%d" % key, [P, width], U8)
             nc.vector.quantize_mx(out=codes[key][:].bitcast(FP8X4), scales=scales[key][:], in_=grouped[key][:])
 
-        def group_h(g, part, copy):
-            interleave(("h", g, part), h_rows[g, part][:], copy, "grouped_h", 3)
+        def group_h(g, part, *copies):
+            interleave(("h", g, part), h_rows[g, part][:], copies, "grouped_h", 3)
 
-        def group_f(g, rg, copy):
-            interleave(("f", g, rg), f_raw[g, rg][:], copy, "grouped_f", 4)
+        def group_f(g, rg, *copies):
+            interleave(("f", g, rg), f_raw[g, rg][:], copies, "grouped_f", 4)
 
         y = {}
         exposure = {}
@@ -308,79 +318,74 @@ def tile_missed_connection_compensation_h2_kernel(
         vec, act = nc.vector.tensor_copy, nc.scalar.copy
 
         turn_slack()
+        warm_up()
         permute_c(0)
         permute_c(1)
         group_f(0, 0, vec)
         permute_c(2)
-        late_wide(0)
         quantize(("f", 0, 0))
         permute_c(3)
+        late_wide(0)
         group_h(0, 0, vec)
+        group_f(1, 0, vec)
         for g in range(1, L_PASSES):
             late_wide(g)
-            if g < L_PASSES - 1:
-                group_f(g, 0, vec)
-            quantize(("h", g - 1, 0))
+            if g == 2:
+                quantize(("f", 1, 0))
             group_h(g, 0, vec)
-            if g < L_PASSES - 1:
-                quantize(("f", g, 0))
+            quantize(("h", g - 1, 0))
+        group_f(2, 0, act)
         group_f(3, 0, act)
+        quantize(("f", 2, 0))
+        quantize(("h", 3, 0))
+        group_f(0, 1, vec)
+        quantize(("f", 3, 0))
         for g in range(L_PASSES):
             late_rest(g)
         turn_liability()
-        quantize(("f", 3, 0))
-        quantize(("h", L_PASSES - 1, 0))
         group_h(0, 1, vec)
-        group_f(0, 1, vec)
-        quantize(("h", 0, 1))
-        group_h(1, 1, vec)
         quantize(("f", 0, 1))
-        for g in range(2, L_PASSES):
+        for g in range(1, L_PASSES):
             group_h(g, 1, vec)
             quantize(("h", g - 1, 1))
-        group_f(3, 1, act)
+        group_f(2, 1, act)
+        group_f(3, 1, act, vec)
         quantize(("h", 3, 1))
         group_f(1, 1, vec)
-        group_f(2, 1, act)
         for i in range(S_TILES):
             product(i, 0)
-        quantize(("f", 3, 1))
-        quantize(("f", 1, 1))
-        finish(0, 0)
-        quantize(("f", 2, 1))
-        finish(1, 0)
-        for g in PASS_ORDER:
-            group_f(g, 2, act)
-        for i in range(4):
+        for g in (2, 1, 3):
+            quantize(("f", g, 1))
+        group_f(0, 2, act)
+        group_f(1, 2, act)
+        for i in range(S_TILES):
+            finish(i, 0)
             product(i, 1)
-            finish(i + 2, 0)
-            if i % 2 == 1:
-                quantize(("f", PASS_ORDER[i // 2], 2))
-        round_y(0, 0, vec)
-        round_y(1, 0, vec)
-        product(4, 1)
-        product(5, 1)
-        quantize(("f", 3, 2))
-        finish(0, 1)
-        finish(1, 1)
-        quantize(("f", 2, 2))
-        for i in range(2, S_TILES):
+            if i == 2:
+                group_f(2, 2, vec)
+                group_f(3, 2, act)
+            if i >= 2:
+                quantize(("f", (0, 2, 1, 3)[i - 2], 2))
+        for i in range(S_TILES):
             round_y(i, 0, act)
         product(0, 2)
-        finish(2, 1)
-        finish(3, 1)
-        finish(4, 1)
+        finish(0, 1)
+        product(1, 2)
+        for i in range(1, 4):
+            finish(i, 1)
+        round_y(0, 1, act)
+        round_y(1, 1, act)
         for i0 in (0, 2, 4):
             turn(i0, 2, 0)
         for i0 in (0, 2, 4):
             collect(i0, 0, act)
+        finish(4, 1)
         finish(5, 1)
-        round_y(0, 1, vec)
-        round_y(1, 1, vec)
-        product(1, 2)
         product(2, 2)
-        for i in range(2, S_TILES):
-            round_y(i, 1, act)
+        round_y(2, 1, act)
+        round_y(3, 1, act)
+        round_y(4, 1, vec)
+        round_y(5, 1, vec)
         finish(0, 2)
         quantize_y(0, 0)
         quantize_y(2, 0)
@@ -388,7 +393,7 @@ def tile_missed_connection_compensation_h2_kernel(
         quantize_y(4, 0)
         store_words(0, 0, S_TILES)
         store_scales(0, [nc.sync])
-        round_y(0, 2, vec)
+        round_y(0, 2, act)
         round_y(1, 2, vec)
         product(3, 2)
         for i0 in (0, 2, 4):
@@ -402,25 +407,25 @@ def tile_missed_connection_compensation_h2_kernel(
         product(4, 2)
         product(5, 2, 0, HALF)
         product(5, 2, HALF, HALF)
-        round_y(2, 2, vec)
-        round_y(3, 2, vec)
+        round_y(2, 2, act)
         quantize_y(0, 1)
+        round_y(3, 2, vec)
         quantize_y(2, 1)
-        quantize_y(4, 1)
-        store_words(1, 0, S_TILES)
-        store_scales(1, [nc.sync])
         finish(4, 2)
+        quantize_y(4, 1)
+        store_scales(1, [nc.sync])
+        store_words(1, 0, S_TILES)
         round_y(4, 2, act)
         finish(5, 2, 0, HALF)
         finish(5, 2, HALF, HALF)
-        turn(2, 2, 2)
-        turn(4, 1, 2)
         round_y(5, 2, vec, 0, HALF)
         round_y(5, 2, vec, HALF, HALF)
+        turn(2, 2, 2)
+        turn(4, 1, 2)
+        turn(5, 1, 2)
         quantize_y(0, 2)
         store_words(2, 0, 2)
         collect(2, 2, act)
-        turn(5, 1, 2)
         collect(4, 2, vec)
         collect(5, 2, act)
         quantize_y(2, 2)

from contextlib import ExitStack

import concourse.mybir as mybir
from concourse.masks import make_identity

S, F, L, R = 768, 1024, 2048, 1536
FLOPS = 2 * S * F * L + 2 * S * L * R

F32 = mybir.dt.float32
BF16 = mybir.dt.bfloat16
I32 = mybir.dt.int32
U32 = mybir.dt.uint32
U8 = mybir.dt.uint8
FP8X4 = mybir.dt.float8_e4m3fn_x4
FP4X4 = mybir.dt.float4_e2m1fn_x4
ALU = mybir.AluOpType
ACT = mybir.ActivationFunctionType

P = 128
KP = 512
F_PASSES = F // KP
L_PASSES = L // KP
R_GROUPS = R // KP
S_TILES = S // P
S_WIDE = 512
S_REST = S - S_WIDE
PASS_ORDER = (0, 1, 2, 3)
WARM_PASSES = 12
HALF = KP // 2


def tile_missed_connection_compensation_h2_kernel(
    tc, delay_words, delay_scales, conn_words, conn_scales, slack, flows, rate, liability, out_0, out_1, out_2
):
    nc = tc.nc
    with ExitStack() as ctx:
        keep = ctx.enter_context(tc.tile_pool(name="keep", bufs=1))
        work = ctx.enter_context(tc.tile_pool(name="work", bufs=1))
        psum = ctx.enter_context(tc.psum_pool(name="psum", bufs=8))
        ctx.enter_context(tc.manual_schedule())

        def kept(name, shape, dtype):
            return keep.tile(shape, dtype, name=name, align_bytes=64)

        def rotating(tag, bufs, shape, dtype):
            return work.tile(shape, dtype, name=tag, tag=tag, bufs=bufs, align_bytes=64)

        def bank(shape, dtype):
            return psum.tile(shape, dtype, name="bank", tag="bank")

        d_scale = kept("d_scale", [P, F_PASSES * S], U8)
        c_scale_first = kept("c_scale_first", [P, F_PASSES, 2 * P], I32)
        c_scale_later = kept("c_scale_later", [P, F_PASSES, 2 * P], I32)
        d_wide = kept("d_wide", [P, F_PASSES, S_WIDE], U32)
        d_rest = kept("d_rest", [P, F_PASSES, S_REST], U32)
        c_raw = [rotating("slab", 18, [P, F_PASSES, 256], I32) for g in range(L_PASSES)]
        c_codes = [kept("c_codes%d" % g, [P, F_PASSES * 1024], U8) for g in range(L_PASSES)]
        c_scale = [kept("c_scale%d" % g, [P, F_PASSES * 512], U8) for g in range(L_PASSES)]
        f_raw = {(g, rg): kept("f_raw%d%d" % (g, rg), [P, 4, KP], BF16) for g in range(L_PASSES) for rg in range(R_GROUPS)}
        slack_rows = kept("slack_rows", [L_PASSES, KP], BF16)
        liab_rows = kept("liab_rows", [P, P], BF16)
        rows = kept("rows", [P, 4, P], BF16)
        neg_slack = kept("neg_slack", [P, 4, L_PASSES], F32)
        liab = kept("liab", [P, S_TILES], F32)
        rate_first = kept("rate_first", [P, KP], BF16)
        rate_later = kept("rate_later", [P, R - KP], BF16)
        warm_codes = kept("warm_codes", [P, P], U32)
        warm_scales = kept("warm_scales", [P, P], U8)
        ident_f32 = kept("ident_f32", [P, P], F32)
        ident_bf16 = kept("ident_bf16", [P, P], BF16)

        nc.vector.memset(rows[:], 0.0)
        nc.vector.memset(d_scale[:].bitcast(I32), 0)
        nc.vector.quantize_mx(
            out=warm_codes[:].bitcast(FP8X4), scales=warm_scales[:], in_=rows[:].rearrange("p t m -> p (t m)")
        )
        nc.vector.memset(c_scale_first[:], 0)
        nc.vector.memset(c_scale_later[:], 0)
        nc.vector.memset(liab_rows[:], 0.0)
        make_identity(nc, ident_f32[:])
        nc.scalar.activation(out=ident_bf16[:], in_=ident_f32[:], func=ACT.Relu)

        def warm_up():
            for n in range(0, WARM_PASSES, 4):
                warm = bank([P, 4, P], F32)
                for j in range(4):
                    nc.tensor.matmul_mx(
                        out=warm[:, j, :],
                        lhsT=warm_codes[:].bitcast(FP8X4),
                        lhsT_scale=warm_scales[:],
                        rhs=warm_codes[:].bitcast(FP8X4),
                        rhs_scale=warm_scales[:],
                        start=True,
                        stop=True,
                    )

        d_words = delay_words.rearrange("g p n t -> p g (n t)").bitcast(I32)
        c_words = conn_words.rearrange("g p b -> p g b").bitcast(I32)
        f_rows = flows.rearrange("(g j t e) r -> g e j t r", g=L_PASSES, t=4, e=4)

        def load_c(queue, g):
            queue.dma_start(out=c_raw[g][:], in_=c_words[:, :, 256 * g : 256 * (g + 1)])

        def load_f(g, rg):
            for e in range(4):
                nc.sync.dma_start(out=f_raw[g, rg][e:P:4, :, :], in_=f_rows[g, e, :, :, KP * rg : KP * (rg + 1)])

        c_sc = conn_scales.rearrange("g q b -> q g b").bitcast(I32)
        d_sc = delay_scales.rearrange("g q b -> q g b").bitcast(I32)

        def load_scales(plane, rows_hbm, r):
            nc.sync.dma_start(out=plane[r:P:32, :, :], in_=rows_hbm[r:16:4, :, :])

        d_plane = d_scale[:].bitcast(I32).rearrange("p (g w) -> p g w", g=F_PASSES)
        nc.sync.dma_start(out=slack_rows[:], in_=slack.rearrange("(g k) -> g k", k=KP))
        load_c(nc.sync, 0)
        load_scales(d_plane, d_sc, 0)
        nc.sync.dma_start(out=d_wide[:].bitcast(I32), in_=d_words[:, :, 0:S_WIDE])
        load_scales(d_plane, d_sc, 1)
        for r in range(4):
            load_scales(c_scale_first, c_sc[:, :, 0 : 2 * P], r)
        for r in range(2, 4):
            load_scales(d_plane, d_sc, r)
        load_c(nc.sync, 1)
        load_f(0, 0)
        for r in range(4):
            load_scales(c_scale_later, c_sc[:, :, 2 * P :], r)
        load_c(nc.sync, 2)
        load_c(nc.sync, 3)
        load_f(1, 0)
        nc.sync.dma_start(out=d_rest[:].bitcast(I32), in_=d_words[:, :, S_WIDE:S])
        load_f(2, 0)
        load_f(3, 0)
        nc.sync.dma_start(out=liab_rows[0:S_TILES, :], in_=liability.rearrange("(i p) -> i p", p=P))
        for g in PASS_ORDER:
            load_f(g, 1)
        nc.sync.dma_start(out=rate_first[:], in_=rate[0:KP].partition_broadcast(P))
        for g in PASS_ORDER:
            load_f(g, 2)
        nc.sync.dma_start(out=rate_later[:], in_=rate[KP:R].partition_broadcast(P))

        def turn_slack():
            nc.vector.tensor_scalar(
                out=rows[0:L_PASSES, :, :].rearrange("g t (j e) -> g t j e", e=4),
                in0=slack_rows[:].rearrange("g (j t e) -> g t j e", t=4, e=4),
                scalar1=-1.0,
                scalar2=None,
                op0=ALU.mult,
            )
            turned = bank([P, 4, P], BF16)
            for t in range(4):
                nc.tensor.transpose(turned[:, t, :], rows[:, t, :], ident_bf16[:])
            nc.scalar.copy(out=neg_slack[:], in_=turned[:, :, 0:L_PASSES])

        def turn_liability():
            turned = bank([P, P], BF16)
            nc.tensor.transpose(turned[:], liab_rows[:], ident_bf16[:])
            nc.scalar.copy(out=liab[:], in_=turned[:, 0:S_TILES])

        def permute_scales(g):
            raw_scale = (c_scale_first if g < 2 else c_scale_later)[:, :, P * (g % 2) : P * (g % 2 + 1)]
            nc.vector.tensor_copy(
                out=c_scale[g][:].bitcast(I32).rearrange("p (f t j) -> p f t j", f=F_PASSES, t=4),
                in_=raw_scale.rearrange("p f (j t) -> p f t j", t=4),
            )

        def permute_codes(g):
            nc.vector.tensor_copy(
                out=c_codes[g][:].bitcast(I32).rearrange("p (f t j h) -> p f t j h", f=F_PASSES, t=4, h=2),
                in_=c_raw[g][:].rearrange("p f (j t h) -> p f t j h", t=4, h=2),
            )

        def permute_c(g):
            permute_codes(g)
            permute_scales(g)

        def late_passes(acc, g, t, d_tile, d_col, s0, width):
            for f in range(F_PASSES):
                nc.tensor.matmul_mx(
                    out=acc,
                    lhsT=c_codes[g][:, 1024 * f + 256 * t : 1024 * f + 256 * (t + 1)].bitcast(FP4X4),
                    lhsT_scale=c_scale[g][:, 512 * f + P * t : 512 * f + P * (t + 1)],
                    rhs=d_tile[:, f, d_col : d_col + width].bitcast(FP8X4),
                    rhs_scale=d_scale[:, S * f + s0 : S * f + s0 + width],
                    start=(f == 0),
                    stop=(f == F_PASSES - 1),
                )

        h_rows = {}

        def late_wide(g):
            h_rows[g, 0] = rotating("h_wide", 3, [P, 4, S_WIDE], BF16)
            for t in range(4):
                acc = bank([P, S_WIDE], F32)
                late_passes(acc[:], g, t, d_wide, 0, 0, S_WIDE)
                nc.scalar.activation(out=h_rows[g, 0][:, t, :], in_=acc[:], func=ACT.Relu, bias=neg_slack[:, t, g : g + 1])

        def late_rest(g):
            h_rows[g, 1] = rotating("h_rest", 4, [P, 4, S_REST], BF16)
            for t0 in (0, 2):
                acc = bank([P, 2, S_REST], F32)
                for t in (t0, t0 + 1):
                    for c in range(0, S_REST, P):
                        late_passes(acc[:, t - t0, c : c + P], g, t, d_rest, c, S_WIDE + c, P)
                for t in (t0, t0 + 1):
                    nc.scalar.activation(
                        out=h_rows[g, 1][:, t, :], in_=acc[:, t - t0, :], func=ACT.Relu, bias=neg_slack[:, t, g : g + 1]
                    )

        grouped = {}
        codes = {}
        scales = {}

        def interleave(key, src, copies, tag, bufs):
            grouped[key] = rotating(tag, bufs, [P, src.shape[2] * 4], BF16)
            width = src.shape[2] // len(copies)
            for n, copy in enumerate(copies):
                copy(
                    out=grouped[key][:, 4 * width * n : 4 * width * (n + 1)].rearrange("p (c i t) -> p c t i", i=4, t=4),
                    in_=src[:, :, width * n : width * (n + 1)].rearrange("p t (c i) -> p c t i", i=4),
                )

        def quantize(key):
            width = grouped[key].shape[1] // 4
            codes[key] = kept("codes_%s%d%d" % key, [P, width], U32)
            scales[key] = kept("scales_%s%d%d" % key, [P, width], U8)
            nc.vector.quantize_mx(out=codes[key][:].bitcast(FP8X4), scales=scales[key][:], in_=grouped[key][:])

        def group_h(g, part, *copies):
            interleave(("h", g, part), h_rows[g, part][:], copies, "grouped_h", 3)

        def group_f(g, rg, *copies):
            interleave(("f", g, rg), f_raw[g, rg][:], copies, "grouped_f", 4)

        y = {}
        exposure = {}

        def product(i, rg, c0=0, width=KP):
            exposure[i, rg, c0] = bank([P, width], F32)
            part, col = (0, P * i) if P * i < S_WIDE else (1, P * i - S_WIDE)
            for n, g in enumerate(PASS_ORDER):
                nc.tensor.matmul_mx(
                    out=exposure[i, rg, c0][:],
                    lhsT=codes["h", g, part][:, col : col + P].bitcast(FP8X4),
                    lhsT_scale=scales["h", g, part][:, col : col + P],
                    rhs=codes["f", g, rg][:, c0 : c0 + width].bitcast(FP8X4),
                    rhs_scale=scales["f", g, rg][:, c0 : c0 + width],
                    start=(n == 0),
                    stop=(n == L_PASSES - 1),
                )

        def finish(i, rg, c0=0, width=KP):
            if c0 == 0:
                y[i, rg] = rotating("slab", 18, [P, KP], F32)
            rate_rg = rate_first[:] if rg == 0 else rate_later[:, KP * (rg - 1) : KP * rg]
            nc.vector.scalar_tensor_tensor(
                out=y[i, rg][:, c0 : c0 + width],
                in0=exposure[i, rg, c0][:],
                scalar=liab[:, i : i + 1],
                in1=rate_rg[:, c0 : c0 + width],
                op0=ALU.mult,
                op1=ALU.mult,
            )
            if c0 + width == KP:
                nc.sync.dma_start(out=out_0[P * i : P * (i + 1), KP * rg : KP * (rg + 1)], in_=y[i, rg][:])

        y_bf16 = {}

        def round_y(i, rg, copy, c0=0, width=KP):
            if c0 == 0:
                y_bf16[i, rg] = rotating("y_bf16", 8, [P, 2, P, 2], BF16)
            copy(
                out=y_bf16[i, rg][:, :, c0 // 4 : (c0 + width) // 4, :],
                in_=y[i, rg][:, c0 : c0 + width].rearrange("s (p u e) -> s u p e", u=2, e=2),
            )

        turned_y = {}
        y_words = {}
        y_codes = [kept("y_codes%d" % rg, [P, S], U32) for rg in range(R_GROUPS)]
        y_scales = [kept("y_scales%d" % rg, [P, S], U8) for rg in range(R_GROUPS)]

        def turn(i0, count, rg):
            turned_y[i0, rg] = bank([P, count, 2, P], F32)
            for ii in range(count):
                words = y_bf16[i0 + ii, rg][:].rearrange("s u p e -> s (u p e)").bitcast(F32)
                for u in range(2):
                    nc.tensor.transpose(turned_y[i0, rg][:, ii, u, :], words[:, P * u : P * (u + 1)], ident_f32[:])

        def collect(i0, rg, copy):
            count = turned_y[i0, rg].shape[1]
            if i0 % 2 == 0:
                y_words[i0 // 2, rg] = rotating("y_words", 4, [P, 2 * KP], BF16)
            c0 = KP * (i0 % 2)
            copy(
                out=y_words[i0 // 2, rg][:, c0 : c0 + KP * count].bitcast(F32).rearrange("p (i s u) -> p i s u", i=count, u=2),
                in_=turned_y[i0, rg][:].rearrange("p i u s -> p i s u"),
            )

        plane_words = out_1.rearrange("g p m t -> g p (m t)").bitcast(I32)
        plane_scales = out_2.bitcast(I32)

        def quantize_y(i0, rg):
            cols = slice(P * i0, P * (i0 + 2))
            nc.vector.quantize_mx(
                out=y_codes[rg][:, cols].bitcast(FP8X4), scales=y_scales[rg][:, cols], in_=y_words[i0 // 2, rg][:]
            )

        def store_words(rg, i0, i1):
            cols = slice(P * i0, P * i1)
            nc.sync.dma_start(out=plane_words[rg, :, cols], in_=y_codes[rg][:, cols].bitcast(I32))

        def store_scales(rg, queues):
            for q in range(4):
                queues[q % len(queues)].dma_start(
                    out=plane_scales[rg, q:16:4, :], in_=y_scales[rg][q:P:32, :].bitcast(I32)
                )

        vec, act = nc.vector.tensor_copy, nc.scalar.copy

        turn_slack()
        warm_up()
        permute_c(0)
        permute_c(1)
        group_f(0, 0, vec)
        permute_c(2)
        quantize(("f", 0, 0))
        permute_c(3)
        late_wide(0)
        group_h(0, 0, vec)
        group_f(1, 0, vec)
        for g in range(1, L_PASSES):
            late_wide(g)
            if g == 2:
                quantize(("f", 1, 0))
            group_h(g, 0, vec)
            quantize(("h", g - 1, 0))
        group_f(2, 0, act)
        group_f(3, 0, act)
        quantize(("f", 2, 0))
        quantize(("h", 3, 0))
        group_f(0, 1, vec)
        quantize(("f", 3, 0))
        for g in range(L_PASSES):
            late_rest(g)
        turn_liability()
        group_h(0, 1, vec)
        quantize(("f", 0, 1))
        for g in range(1, L_PASSES):
            group_h(g, 1, vec)
            quantize(("h", g - 1, 1))
        group_f(2, 1, act)
        group_f(3, 1, act, vec)
        quantize(("h", 3, 1))
        group_f(1, 1, vec)
        for i in range(S_TILES):
            product(i, 0)
        for g in (2, 1, 3):
            quantize(("f", g, 1))
        group_f(0, 2, act)
        group_f(1, 2, act)
        for i in range(S_TILES):
            finish(i, 0)
            product(i, 1)
            if i == 2:
                group_f(2, 2, vec)
                group_f(3, 2, act)
            if i >= 2:
                quantize(("f", (0, 2, 1, 3)[i - 2], 2))
        for i in range(S_TILES):
            round_y(i, 0, act)
        product(0, 2)
        finish(0, 1)
        product(1, 2)
        for i in range(1, 4):
            finish(i, 1)
        round_y(0, 1, act)
        round_y(1, 1, act)
        for i0 in (0, 2, 4):
            turn(i0, 2, 0)
        for i0 in (0, 2, 4):
            collect(i0, 0, act)
        finish(4, 1)
        finish(5, 1)
        product(2, 2)
        round_y(2, 1, act)
        round_y(3, 1, act)
        round_y(4, 1, vec)
        round_y(5, 1, vec)
        finish(0, 2)
        quantize_y(0, 0)
        quantize_y(2, 0)
        finish(1, 2)
        quantize_y(4, 0)
        store_words(0, 0, S_TILES)
        store_scales(0, [nc.sync])
        round_y(0, 2, act)
        round_y(1, 2, vec)
        product(3, 2)
        for i0 in (0, 2, 4):
            turn(i0, 2, 1)
        turn(0, 2, 2)
        finish(2, 2)
        for i0 in (0, 2, 4):
            collect(i0, 1, act)
        collect(0, 2, act)
        finish(3, 2)
        product(4, 2)
        product(5, 2, 0, HALF)
        product(5, 2, HALF, HALF)
        round_y(2, 2, act)
        quantize_y(0, 1)
        round_y(3, 2, vec)
        quantize_y(2, 1)
        finish(4, 2)
        quantize_y(4, 1)
        store_scales(1, [nc.sync])
        store_words(1, 0, S_TILES)
        round_y(4, 2, act)
        finish(5, 2, 0, HALF)
        finish(5, 2, HALF, HALF)
        round_y(5, 2, vec, 0, HALF)
        round_y(5, 2, vec, HALF, HALF)
        turn(2, 2, 2)
        turn(4, 1, 2)
        turn(5, 1, 2)
        quantize_y(0, 2)
        store_words(2, 0, 2)
        collect(2, 2, act)
        collect(4, 2, vec)
        collect(5, 2, act)
        quantize_y(2, 2)
        store_words(2, 2, 4)
        quantize_y(4, 2)
        store_words(2, 4, S_TILES)
        store_scales(2, [nc.sync])
